import numpy as np
import ml_dtypes


def mxq(x, axis, fmt="e4m3"):
    dtype, down = {"e4m3": (ml_dtypes.float8_e4m3fn, 7), "e5m2": (ml_dtypes.float8_e5m2, 14)}[fmt]
    v = np.moveaxis(np.asarray(x, np.float32).astype(ml_dtypes.bfloat16).astype(np.float64), axis, -1)
    blocks = v.reshape(v.shape[:-1] + (-1, 32))
    amax = np.abs(blocks).max(-1, keepdims=True)
    byte = np.maximum(np.where(amax > 0, np.frexp(amax)[1] - 1 + 127, 0) - down, 1)
    scale = np.exp2(byte - 127.0)
    codes = (blocks / scale).astype(np.float32).astype(dtype).astype(np.float64)
    return np.moveaxis((codes * scale).reshape(v.shape), -1, axis)


WIDE = False


def mx_kscale(k):
    if not WIDE:
        return np.ones(k)
    levels = np.array([10, -10, 5, -5, 0])
    if k % 512:
        return np.exp2(np.random.permutation(np.resize(levels, k // 32))).repeat(32)
    a = np.empty((k // 512, 16))
    for p in range(k // 512):
        a[p, :8] = np.random.permutation(np.resize(levels, 8))
        for g in range(8):
            far = levels[np.abs(levels - a[p, g]) >= 10]
            a[p, g + 8] = far[np.random.randint(len(far))]
    return np.exp2(a.ravel()).repeat(32)


BF16 = ml_dtypes.bfloat16


def bf(x):
    return np.asarray(x, np.float32).astype(BF16)


def f64(x):
    return np.asarray(x).astype(np.float64)


E2M1 = np.array([0.0, 0.5, 1.0, 1.5, 2.0, 3.0, 4.0, 6.0, -0.0, -0.5, -1.0, -1.5, -2.0, -3.0, -4.0, -6.0])


def pack_weight(w, fmt):
    k, n = w.shape
    w = f64(bf(w)).reshape(k // 32, 32, n)
    amax = np.abs(w).max(1)
    if fmt == "e4m3":
        byte = np.frexp(amax)[1] - 1 + 127 - 7
    else:
        mant, ex = np.frexp(amax / 6.0)
        byte = np.where(mant > 0.5, ex, ex - 1) + 127
    byte = np.clip(np.where(amax > 0, byte, 1), 1, 254)
    scaled = (w * np.exp2(127.0 - byte)[:, None, :]).reshape(k, n).astype(np.float32)
    by_word = np.ascontiguousarray(scaled.reshape(k // 512, 128, 4, n).transpose(0, 1, 3, 2))
    if fmt == "e4m3":
        words = by_word.astype(ml_dtypes.float8_e4m3fn).view(np.uint8)
    else:
        c = by_word.astype(ml_dtypes.float4_e2m1fn).view(np.uint8) & 0xF
        words = c[..., 0::2] | (c[..., 1::2] << 4)
    return np.ascontiguousarray(words), np.ascontiguousarray(byte.astype(np.uint8).reshape(k // 512, 16, n))


def unpack_weight(words, scales, fmt):
    g, p, n, _ = words.shape
    if fmt == "e4m3":
        vals = np.ascontiguousarray(words).view(ml_dtypes.float8_e4m3fn).astype(np.float64)
    else:
        nib = np.empty((g, p, n, 4), np.uint8)
        nib[..., 0::2] = words & 0xF
        nib[..., 1::2] = words >> 4
        vals = E2M1[nib]
    vals = vals * np.repeat(np.exp2(scales.astype(np.float64) - 127.0), 8, axis=1)[..., None]
    return vals.transpose(0, 1, 3, 2).reshape(g * 512, n)
def pack4(w):
    words, scales = pack_weight(w, "e2m1")
    return words.reshape(words.shape[0], 128, -1), scales


def unpack4(words, scales):
    return unpack_weight(words.reshape(words.shape[0], 128, -1, 2), scales, "e2m1")


def planes(Y):
    n, m = Y.shape
    b = f64(bf(Y)).reshape(n // 32, 32, m)
    amax = np.abs(b).max(1)
    byte = np.clip(np.where(amax > 0, np.frexp(amax)[1] - 1 + 127 - 7, 1), 1, 254)
    codes = (b * np.exp2(127.0 - byte)[:, None, :]).reshape(n, m).astype(np.float32).astype(ml_dtypes.float8_e4m3fn).view(np.uint8)
    words = codes.reshape(n // 512, 128, 4, m).transpose(0, 1, 3, 2)
    return np.ascontiguousarray(words), np.ascontiguousarray(byte.astype(np.uint8).reshape(n // 512, 16, m))


D, K, J, M = 1536, 1024, 1024, 512

def setup_inputs():
    rn = np.random.randn
    s, t, v = mx_kscale(K), mx_kscale(D), mx_kscale(J)
    A = rn(K, D) / np.sqrt(K)
    L_words, L_scales = pack4(A / s[:, None])
    R = bf(A * s[:, None] * t[None, :])
    B = rn(D, D)
    H = bf(0.5 * (B + B.T) / np.sqrt(D) * t[None, :])
    size = np.exp(0.8 * rn(D))
    X = size[None, :] * np.exp(0.8 * rn(J, D))
    X = X / X.mean(axis=1, keepdims=True)
    X_words, X_scales = pack_weight(X * v[:, None] / t[None, :], "e4m3")
    E = np.exp(2.0 * rn(J, M))
    W = bf(0.8 * E / E.sum(axis=0, keepdims=True) / v[:, None])
    anchor = bf(0.2 * np.exp(0.5 * rn(D)) / t)
    Z = bf(size[:, None] * np.exp(0.3 * rn(D, M)))
    rate = bf(0.25 * np.exp(0.3 * rn(M)))
    shift = bf(0.3 * rn(M))
    return dict(L_words=L_words, L_scales=L_scales, R=R, H=H, X_words=X_words, X_scales=X_scales,
                W=W, anchor=anchor, Z=Z, rate=rate, shift=shift)

def reference(L_words, L_scales, R, H, X_words, X_scales, W, anchor, Z, rate, shift):
    L = unpack4(L_words, L_scales)
    X = unpack_weight(X_words, X_scales, "e4m3")
    Q = (L.T @ mxq(f64(R), 0, "e4m3")) + f64(H)
    U = (X.T @ mxq(f64(W), 0, "e4m3")) + f64(anchor)[:, None]
    V = mxq(Q, 1, "e4m3") @ mxq(U, 0, "e4m3")
    y = f64(Z) * np.exp(f64(shift)[None, :] - f64(rate)[None, :] * V)
    Y = y
    words, scales = planes(Y)
    return y, words, scales

@@ -1,0 +1,413 @@
+from contextlib import ExitStack
+
+import concourse.mybir as mybir
+from concourse.masks import make_identity
+
+D, K, J, M = 1536, 1024, 1024, 512
+FLOPS = 2 * D * K * D + 2 * D * J * M + 2 * D * D * M
+
+F32 = mybir.dt.float32
+BF16 = mybir.dt.bfloat16
+I32 = mybir.dt.int32
+U32 = mybir.dt.uint32
+U8 = mybir.dt.uint8
+FP8X4 = mybir.dt.float8_e4m3fn_x4
+FP4X4 = mybir.dt.float4_e2m1fn_x4
+ALU = mybir.AluOpType
+ACT = mybir.ActivationFunctionType
+
+P = 128
+G = 512
+PASSES = K // G
+GROUPS = D // G
+TILES = G // P
+HEAD_V = 336
+U_V = 256
+W_ENG = "s"
+Y_ENG = "v"
+MM_BANKS = 5
+SIDE_V = 0
+SIDE_W = 0
+SIDE_V2 = 0
+RUN = 2
+Y_LAST = 8
+
+
+def tile_multiplicative_quadratic_step_k4_kernel(
+    tc, L_words, L_scales, R, H, X_words, X_scales, W, anchor, Z, rate, shift, out_0, out_1, out_2
+):
+    nc = tc.nc
+    with ExitStack() as ctx:
+        keep = ctx.enter_context(tc.tile_pool(name="keep", bufs=1))
+        work = ctx.enter_context(tc.tile_pool(name="work", bufs=4))
+        psum = ctx.enter_context(tc.psum_pool(name="psum", bufs=1))
+        ctx.enter_context(tc.manual_schedule())
+
+        r_raw, w_raw, h_raw, x_raw, z_raw, l_codes = {}, {}, {}, {}, {}, {}
+        q_acc = {}
+        r_mx, w_mx, q_mx, u_mx, y_mx = {}, {}, {}, {}, {}
+        x_codes, q_rows, q_packed, u_rows, u_packed, e_rows, y_rows, y_packed, packed = {}, {}, {}, {}, {}, {}, {}, {}, {}
+
+        def load_rows(name, rows, tag=None):
+            t = keep.tile([P, 4, G], BF16, name=name, tag=tag or name)
+            nc.sync.dma_start(out=t[:], in_=rows)
+            return t
+
+        def load_r(c, g):
+            rows = R[c * G : (c + 1) * G, g * G : (g + 1) * G]
+            r_raw[c, g] = load_rows("r_raw_%d_%d" % (c, g), rows.rearrange("(p t) n -> p t n", t=4))
+
+        def load_w(c):
+            w_raw[c] = load_rows("w_raw_%d" % c, W[c * G : (c + 1) * G, :].rearrange("(p t) n -> p t n", t=4))
+
+        def load_z(a):
+            z_raw[a] = load_rows("z_raw_%d" % a, Z[a * G : (a + 1) * G, :].rearrange("(p t) n -> p t n", t=4), "r_raw_0_%d" % a)
+
+        def load_h(a, g):
+            rows = H[a * G : (a + 1) * G, g * G : (g + 1) * G]
+            h_raw[a, g] = load_rows("h_raw_%d_%d" % (a, g), rows.rearrange("(i p) n -> p i n", p=P))
+
+        def load_l(a):
+            t = keep.tile([P, PASSES, 2 * G], U8, name="l_codes_%d" % a, align_bytes=64)
+            src = L_words[:, :, 2 * a * G : 2 * (a + 1) * G].rearrange("c p n -> p c n")
+            nc.sync.dma_start(out=t[:].bitcast(I32), in_=src.bitcast(I32))
+            l_codes[a] = t
+
+        def load_x(g):
+            t = keep.tile([P, PASSES, G], I32, name="x_raw_%d" % g)
+            src = X_words.rearrange("c p n t -> p c (n t)")[:, :, 4 * g * G : 4 * (g + 1) * G]
+            nc.sync.dma_start(out=t[:], in_=src.bitcast(I32))
+            x_raw[g] = t
+
+        def load_scale_rows(queue, plane, scales):
+            for quad in range(4):
+                src = scales[:, 4 * quad : 4 * quad + 4, :].rearrange("c r n -> r c n")
+                queue.dma_start(out=plane[32 * quad : 32 * quad + 4, :, :].bitcast(I32), in_=src.bitcast(I32))
+
+        def interleave(engine, dst, src, lo, hi):
+            out = dst[:, 4 * lo : 4 * hi].rearrange("p (c i t) -> p c t i", i=4, t=4)
+            in_ = src[:, :, lo:hi].rearrange("p t (c i) -> p c t i", i=4)
+            if engine == "v":
+                nc.vector.tensor_copy(out=out, in_=in_)
+            elif engine == "s":
+                nc.scalar.copy(out=out, in_=in_)
+            else:
+                nc.gpsimd.tensor_scalar(out=out, in0=in_, scalar1=1.0, scalar2=0.0, op0=ALU.mult, op1=ALU.add)
+
+        def new_packed(name):
+            return work.tile([P, 4 * G], BF16, name=name, tag="packed", bufs=5, align_bytes=64)
+
+        def new_mx(name):
+            codes = keep.tile([P, G], U32, name=name + "_codes", align_bytes=64)
+            scales = keep.tile([P, G], U8, name=name + "_scales", align_bytes=64)
+            return codes, scales
+
+        def quantize(name, src):
+            codes, scales = new_mx(name)
+            nc.vector.quantize_mx(out=codes[:].bitcast(FP8X4), scales=scales[:], in_=src[:])
+            return codes, scales
+
+        def mm_bank(name):
+            return psum.tile([P, G], F32, name=name, tag="mm", bufs=MM_BANKS)
+
+        def turn_bank(name):
+            return psum.tile([P, 4, P], F32, name=name, tag="turn", bufs=8 - MM_BANKS)
+
+        def pack(key, raw, on_vector, other="s"):
+            packed[key] = new_packed("packed_%s_%d_%d" % key)
+            if on_vector < G:
+                interleave(other, packed[key], raw, on_vector, G)
+            if on_vector > 0:
+                interleave("v", packed[key], raw, 0, on_vector)
+
+        def quant_r(c, g):
+            r_mx[c, g] = quantize("r_%d_%d" % (c, g), packed["r", c, g])
+
+        def quant_w(c):
+            w_mx[c] = quantize("w_%d" % c, packed["w", c, 0])
+
+        def q_pass(a, g, i, c):
+            if c == 0:
+                q_acc[a, g, i] = mm_bank("q_acc_%d_%d_%d" % (a, g, i))
+            acc = q_acc[a, g, i]
+            nc.tensor.matmul_mx(
+                out=acc[:],
+                lhsT=l_codes[a][:, c, 2 * i * P : 2 * (i + 1) * P].bitcast(FP4X4),
+                lhsT_scale=l_scales[:, c, a * G + i * P : a * G + (i + 1) * P],
+                rhs=r_mx[c, g][0][:].bitcast(FP8X4),
+                rhs_scale=r_mx[c, g][1][:],
+                start=(c == 0),
+                stop=(c == PASSES - 1),
+            )
+
+        def q_tile(a, g, i):
+            for c in range(PASSES):
+                q_pass(a, g, i, c)
+            q_add(a, g, i)
+
+        def q_add(a, g, i):
+            acc = q_acc[a, g, i]
+            rows = work.tile([P, G], BF16, name="q_rows_%d_%d_%d" % (a, g, i), tag="q_rows", bufs=8)
+            nc.vector.tensor_tensor(
+                out=rows[:].rearrange("p (u j e) -> p u j e", u=2, e=2),
+                in0=acc[:].rearrange("p (j u e) -> p u j e", u=2, e=2),
+                in1=h_raw[a, g][:, i, :].rearrange("p (j u e) -> p u j e", u=2, e=2),
+                op=ALU.add,
+            )
+            q_rows[a, g, i] = rows
+
+        def q_turn(a, g, half):
+            bank = turn_bank("q_turn_%d_%d_%d" % (a, g, half))
+            for i in range(2):
+                words = q_rows[a, g, 2 * half + i][:].bitcast(F32)
+                for u in range(2):
+                    nc.tensor.transpose(bank[:, 2 * i + u, :], words[:, u * P : (u + 1) * P], ident[:])
+            if half == 0:
+                q_packed[a, g] = new_packed("q_packed_%d_%d" % (a, g))
+            dst = q_packed[a, g][:].bitcast(F32).rearrange("p (t i j u) -> p t i j u", t=4, i=4, u=2)
+            nc.scalar.copy(
+                out=dst[:, :, 2 * half : 2 * half + 2, :, :],
+                in_=bank[:].rearrange("p (i u) (j t) -> p t i j u", u=2, t=4),
+            )
+
+        def q_quant(a, g):
+            q_mx[a, g] = quantize("q_%d_%d" % (a, g), q_packed[a, g])
+
+        def x_sort(g):
+            t = keep.tile([P, PASSES, G], I32, name="x_codes_%d" % g, align_bytes=64)
+            nc.vector.tensor_copy(
+                out=t[:].rearrange("p c (t j i) -> p c j t i", t=4, i=4),
+                in_=x_raw[g][:].rearrange("p c (j i t) -> p c j t i", t=4, i=4),
+            )
+            s = keep.tile([P, PASSES, G], U8, name="x_scales_%d" % g, align_bytes=64)
+            nc.vector.tensor_copy(
+                out=s[:].rearrange("p c (t j i) -> p c j t i", t=4, i=16),
+                in_=x_plane[:, :, g * G : (g + 1) * G].rearrange("p c (j i t) -> p c j t i", t=4, i=16),
+            )
+            x_codes[g] = (t, s)
+
+        def u_tile(g, t):
+            acc = mm_bank("u_acc_%d_%d" % (g, t))
+            for c in range(PASSES):
+                nc.tensor.matmul_mx(
+                    out=acc[:],
+                    lhsT=x_codes[g][0][:, c, t * P : (t + 1) * P].bitcast(FP8X4),
+                    lhsT_scale=x_codes[g][1][:, c, t * P : (t + 1) * P],
+                    rhs=w_mx[c][0][:].bitcast(FP8X4),
+                    rhs_scale=w_mx[c][1][:],
+                    start=(c == 0),
+                    stop=(c == PASSES - 1),
+                )
+            if t == 0:
+                u_rows[g] = work.tile([P, 4, M], BF16, name="u_rows_%d" % g, tag="u_rows", bufs=2)
+            nc.scalar.activation(out=u_rows[g][:, t, :], in_=acc[:], func=ACT.Identity, bias=anchor_sb[:, g, t : t + 1])
+
+        def u_quant(g):
+            u_mx[g] = quantize("u_%d" % g, packed["u", g, 0])
+
+        def v_tile(a, mt):
+            acc = mm_bank("v_acc_%d_%d" % (a, mt))
+            cols = slice(mt * P, (mt + 1) * P)
+            for g in range(GROUPS):
+                nc.tensor.matmul_mx(
+                    out=acc[:],
+                    lhsT=u_mx[g][0][:, cols].bitcast(FP8X4),
+                    lhsT_scale=u_mx[g][1][:, cols],
+                    rhs=q_mx[a, g][0][:].bitcast(FP8X4),
+                    rhs_scale=q_mx[a, g][1][:],
+                    start=(g == 0),
+                    stop=(g == GROUPS - 1),
+                )
+            rows = work.tile([P, G], F32, name="e_rows_%d_%d" % (a, mt), tag="e_rows", bufs=6)
+            nc.scalar.activation(
+                out=rows[:], in_=acc[:], func=ACT.Exp, bias=coef[:, 32 + mt : 33 + mt], scale=coef[:, mt : mt + 1]
+            )
+            e_rows[a, mt] = rows
+
+        def e_turn(a, mt):
+            bank = turn_bank("e_turn_%d_%d" % (a, mt))
+            for t in range(4):
+                nc.tensor.transpose(bank[:, t, :], e_rows[a, mt][:, t * P : (t + 1) * P], ident[:])
+            cols = slice(mt * P, (mt + 1) * P)
+            if mt % 2 == 0:
+                y_rows[a, mt // 2] = work.tile([P, 4, 2 * P], F32, name="y_rows_%d_%d" % (a, mt), tag="y_rows", bufs=3)
+            rows = y_rows[a, mt // 2]
+            half = slice((mt % 2) * P, (mt % 2 + 1) * P)
+            nc.vector.tensor_tensor(out=rows[:, :, half], in0=bank[:], in1=z_raw[a][:, :, cols], op=ALU.mult)
+            if (a, mt // 2) == (GROUPS - 1, 1):
+                dst = out_0[a * G : (a + 1) * G, cols].rearrange("(p t) m -> p t m", t=4)
+                nc.sync.dma_start(out=dst, in_=rows[:, :, half])
+            elif mt % 2 == 1:
+                dst = out_0[a * G : (a + 1) * G, (mt - 1) * P : (mt + 1) * P].rearrange("(p t) m -> p t m", t=4)
+                nc.sync.dma_start(out=dst, in_=rows[:])
+
+        def y_pack(a, mt, engine):
+            t = work.tile([P, 4 * P], BF16, name="y_packed_%d_%d" % (a, mt), tag="y_packed", bufs=4, align_bytes=64)
+            interleave(engine, t, y_rows[a, mt // 2][:, :, (mt % 2) * P : (mt % 2 + 1) * P], 0, P)
+            y_packed[a, mt] = t
+
+        def y_quant(a, mt):
+            if mt == 0:
+                y_mx[a] = new_mx("y_%d" % a)
+            codes, scales = y_mx[a]
+            cols = slice(mt * P, (mt + 1) * P)
+            nc.vector.quantize_mx(out=codes[:, cols].bitcast(FP8X4), scales=scales[:, cols], in_=y_packed[a, mt][:])
+            if mt % 2 == 1:
+                dst = out_1[a, :, (mt - 1) * P : (mt + 1) * P, :].rearrange("p m t -> p (m t)")
+                nc.sync.dma_start(out=dst.bitcast(I32), in_=codes[:, (mt - 1) * P : (mt + 1) * P].bitcast(I32))
+            if mt == TILES - 1:
+                for quad in range(4):
+                    queue = nc.scalar if a == GROUPS - 1 and quad % 2 == 1 else nc.sync
+                    queue.dma_start(
+                        out=out_2[a, 4 * quad : 4 * quad + 4, :].bitcast(I32),
+                        in_=scales[32 * quad : 32 * quad + 4, :].bitcast(I32),
+                    )
+
+        l_scales = keep.tile([P, PASSES, D], U8, name="l_scales", align_bytes=64)
+        x_plane = keep.tile([P, PASSES, D], U8, name="x_plane", align_bytes=64)
+        nc.vector.memset(l_scales[:].bitcast(I32), 0)
+        warm = keep.tile([P, 2], F32, name="warm")
+        nc.vector.memset(warm[:, 0:1], 0.0)
+        nc.vector.memset(x_plane[:].bitcast(I32), 0)
+        load_r(0, 0)
+        load_scale_rows(nc.scalar, l_scales, L_scales)
+        load_l(0)
+        load_r(1, 0)
+        load_h(0, 0)
+
+        ident = keep.tile([P, P], F32, name="ident")
+        coef_bf = keep.tile([P, P], BF16, name="coef_bf")
+        coef_rows = keep.tile([P, P], F32, name="coef_rows")
+        anchor_sb = keep.tile([P, GROUPS, 4], BF16, name="anchor_sb")
+        nc.gpsimd.dma_start(out=coef_bf[0:4, :], in_=rate.rearrange("(i p) -> i p", p=P))
+        nc.gpsimd.dma_start(out=coef_bf[32:36, :], in_=shift.rearrange("(i p) -> i p", p=P))
+        nc.gpsimd.dma_start(out=anchor_sb[:], in_=anchor.rearrange("(g p t) -> p g t", p=P, t=4))
+        nc.gpsimd.memset(coef_rows[:], 0.0)
+        nc.scalar.activation(out=warm[:, 1:2], in_=warm[:, 0:1], func=ACT.Exp)
+        make_identity(nc, ident[:])
+        nc.gpsimd.tensor_scalar(
+            out=coef_rows[0:4, :], in0=coef_bf[0:4, :], scalar1=-1.0, scalar2=0.0, op0=ALU.mult, op1=ALU.add
+        )
+        nc.gpsimd.tensor_scalar(
+            out=coef_rows[32:36, :], in0=coef_bf[32:36, :], scalar1=1.0, scalar2=0.0, op0=ALU.mult, op1=ALU.add
+        )
+
+        load_r(0, 1)
+        load_l(1)
+        load_h(1, 0)
+        load_r(1, 1)
+        load_l(2)
+        load_h(2, 0)
+        load_w(0)
+        load_h(0, 1)
+        load_w(1)
+        load_scale_rows(nc.sync, x_plane, X_scales)
+        load_h(1, 1)
+        load_x(0)
+        load_r(0, 2)
+        load_h(2, 1)
+        load_r(1, 2)
+        load_x(1)
+        load_h(0, 2)
+        load_x(2)
+        load_h(1, 2)
+        load_h(2, 2)
+
+        coef = keep.tile([P, 36], F32, name="coef")
+
+        def make_coef():
+            bank = turn_bank("coef_turn")
+            nc.tensor.transpose(bank[:, 0, :], coef_rows[:], ident[:])
+            nc.scalar.copy(out=coef[:], in_=bank[:, 0, 0:36])
+
+        def u_group(g):
+            for t in range(4):
+                u_tile(g, t)
+
+        def u_pack_s(g):
+            packed["u", g, 0] = new_packed("packed_u_%d" % g)
+            interleave("s", packed["u", g, 0], u_rows[g], U_V, G)
+
+        def u_pack_v(g):
+            if U_V > 0:
+                interleave("v", packed["u", g, 0], u_rows[g], 0, U_V)
+
+        def turn(a, g):
+            q_turn(a, g, 0)
+            q_turn(a, g, 1)
+
+        def unit(a, g, side=()):
+            side = list(side)
+            for i in range(TILES):
+                q_tile(a, g, i)
+                if i < len(side) and side[i] is not None:
+                    side[i]()
+
+        for c in range(PASSES):
+            pack(("r", c, 0), r_raw[c, 0], HEAD_V)
+            quant_r(c, 0)
+            for i in range(TILES):
+                q_pass(0, 0, i, c)
+        pack(("r", 0, 1), r_raw[0, 1], SIDE_V)
+        for i in range(TILES):
+            q_add(0, 0, i)
+        unit(1, 0, [None, lambda: quant_r(0, 1)])
+        pack(("r", 1, 1), r_raw[1, 1], SIDE_V)
+        turn(0, 0)
+        make_coef()
+        unit(2, 0, [None, lambda: quant_r(1, 1), None, lambda: q_quant(0, 0)])
+        pack(("w", 0, 0), w_raw[0], SIDE_W, W_ENG)
+        turn(1, 0)
+        unit(0, 1, [None, lambda: quant_w(0), None, lambda: q_quant(1, 0)])
+        pack(("w", 1, 0), w_raw[1], SIDE_W, W_ENG)
+        turn(2, 0)
+        unit(1, 1, [None, lambda: quant_w(1), lambda: x_sort(0), lambda: q_quant(2, 0)])
+        pack(("r", 0, 2), r_raw[0, 2], SIDE_V)
+        turn(0, 1)
+        unit(2, 1, [None, lambda: quant_r(0, 2), None, lambda: q_quant(0, 1)])
+        pack(("r", 1, 2), r_raw[1, 2], SIDE_V2)
+        for a in range(GROUPS):
+            load_z(a)
+        turn(1, 1)
+        u_group(0)
+        x_sort(1)
+        quant_r(1, 2)
+        q_quant(1, 1)
+        turn(2, 1)
+        u_pack_s(0)
+        unit(0, 2, [None, lambda: u_pack_v(0), lambda: q_quant(2, 1), lambda: u_quant(0)])
+        u_group(1)
+        x_sort(2)
+        turn(0, 2)
+        u_pack_s(1)
+        unit(1, 2, [None, lambda: u_pack_v(1), lambda: q_quant(0, 2), lambda: u_quant(1)])
+        u_group(2)
+        u_pack_s(2)
+        turn(1, 2)
+        u_pack_v(2)
+        unit(2, 2, [lambda: u_quant(2), None, lambda: q_quant(1, 2)])
+
+        steps = [(a, mt) for a in range(GROUPS) for mt in range(TILES)]
+
+        def finish(pair):
+            for step in pair:
+                e_turn(*step)
+            for step in pair:
+                y_pack(*step, "s" if step[1] % 2 == 0 else "v")
+            for step in pair:
+                y_quant(*step)
+
+        pairs = [steps[s : s + 2] for s in range(0, len(steps), 2)]
+        for n, pair in enumerate(pairs[:-1]):
+            for step in pair:
+                v_tile(*step)
+            if n == 0:
+                turn(2, 2)
+            else:
+                finish(pairs[n - 1])
+            if n == 1:
+                q_quant(2, 2)
+        v_tile(*pairs[-1][0])
+        finish(pairs[-2])
+        v_tile(*pairs[-1][1])
+        finish(pairs[-1])

@@ -26,9 +26,15 @@ U_V = 256
 W_ENG = "s"
 Y_ENG = "v"
 MM_BANKS = 5
+HEAD_TILES = 2
+HALF = M // 2
+ANCHOR_COL = 64
+UE0 = "s"
+UE1 = "v"
+YE = "s"
 SIDE_V = 0
 SIDE_W = 0
-SIDE_V2 = 0
+SIDE_V2 = 128
 RUN = 2
 Y_LAST = 8
 
@@ -43,13 +49,15 @@ def tile_multiplicative_quadratic_step_k4_kernel(
         psum = ctx.enter_context(tc.psum_pool(name="psum", bufs=1))
         ctx.enter_context(tc.manual_schedule())
 
-        r_raw, w_raw, h_raw, x_raw, z_raw, l_codes = {}, {}, {}, {}, {}, {}
+        r_raw, h_raw, x_raw, z_raw, l_codes = {}, {}, {}, {}, {}
+        w_raw = keep.tile([P, PASSES, 4, M], BF16, name="w_raw")
+        x_sorted = keep.tile([P, PASSES, D], U8, name="x_sorted", align_bytes=64)
         q_acc = {}
         r_mx, w_mx, q_mx, u_mx, y_mx = {}, {}, {}, {}, {}
         x_codes, q_rows, q_packed, u_rows, u_packed, e_rows, y_rows, y_packed, packed = {}, {}, {}, {}, {}, {}, {}, {}, {}
 
         def load_rows(name, rows, tag=None):
-            t = keep.tile([P, 4, G], BF16, name=name, tag=tag or name)
+            t = keep.tile([P, 4, G], BF16, name=name, tag=tag or name, align_bytes=64)
             nc.sync.dma_start(out=t[:], in_=rows)
             return t
 
@@ -57,8 +65,8 @@ def tile_multiplicative_quadratic_step_k4_kernel(
             rows = R[c * G : (c + 1) * G, g * G : (g + 1) * G]
             r_raw[c, g] = load_rows("r_raw_%d_%d" % (c, g), rows.rearrange("(p t) n -> p t n", t=4))
 
-        def load_w(c):
-            w_raw[c] = load_rows("w_raw_%d" % c, W[c * G : (c + 1) * G, :].rearrange("(p t) n -> p t n", t=4))
+        def load_w():
+            nc.sync.dma_start(out=w_raw[:], in_=W.rearrange("(c p t) n -> p c t n", p=P, t=4))
 
         def load_z(a):
             z_raw[a] = load_rows("z_raw_%d" % a, Z[a * G : (a + 1) * G, :].rearrange("(p t) n -> p t n", t=4), "r_raw_0_%d" % a)
@@ -79,9 +87,9 @@ def tile_multiplicative_quadratic_step_k4_kernel(
             nc.sync.dma_start(out=t[:], in_=src.bitcast(I32))
             x_raw[g] = t
 
-        def load_scale_rows(queue, plane, scales):
+        def load_scale_rows(queue, plane, scales, cols):
             for quad in range(4):
-                src = scales[:, 4 * quad : 4 * quad + 4, :].rearrange("c r n -> r c n")
+                src = scales[:, 4 * quad : 4 * quad + 4, cols].rearrange("c r n -> r c n")
                 queue.dma_start(out=plane[32 * quad : 32 * quad + 4, :, :].bitcast(I32), in_=src.bitcast(I32))
 
         def interleave(engine, dst, src, lo, hi):
@@ -95,7 +103,7 @@ def tile_multiplicative_quadratic_step_k4_kernel(
                 nc.gpsimd.tensor_scalar(out=out, in0=in_, scalar1=1.0, scalar2=0.0, op0=ALU.mult, op1=ALU.add)
 
         def new_packed(name):
-            return work.tile([P, 4 * G], BF16, name=name, tag="packed", bufs=5, align_bytes=64)
+            return work.tile([P, 4 * G], BF16, name=name, tag="packed", bufs=3, align_bytes=64)
 
         def new_mx(name):
             codes = keep.tile([P, G], U32, name=name + "_codes", align_bytes=64)
@@ -123,8 +131,10 @@ def tile_multiplicative_quadratic_step_k4_kernel(
         def quant_r(c, g):
             r_mx[c, g] = quantize("r_%d_%d" % (c, g), packed["r", c, g])
 
-        def quant_w(c):
-            w_mx[c] = quantize("w_%d" % c, packed["w", c, 0])
+        def l_scale_cols(a, c, i):
+            if a == 0:
+                return l_first[:, c, i * P : (i + 1) * P]
+            return l_rest[:, c, (a - 1) * G + i * P : (a - 1) * G + (i + 1) * P]
 
         def q_pass(a, g, i, c):
             if c == 0:
@@ -133,7 +143,7 @@ def tile_multiplicative_quadratic_step_k4_kernel(
             nc.tensor.matmul_mx(
                 out=acc[:],
                 lhsT=l_codes[a][:, c, 2 * i * P : 2 * (i + 1) * P].bitcast(FP4X4),
-                lhsT_scale=l_scales[:, c, a * G + i * P : a * G + (i + 1) * P],
+                lhsT_scale=l_scale_cols(a, c, i),
                 rhs=r_mx[c, g][0][:].bitcast(FP8X4),
                 rhs_scale=r_mx[c, g][1][:],
                 start=(c == 0),
@@ -149,9 +159,9 @@ def tile_multiplicative_quadratic_step_k4_kernel(
             acc = q_acc[a, g, i]
             rows = work.tile([P, G], BF16, name="q_rows_%d_%d_%d" % (a, g, i), tag="q_rows", bufs=8)
             nc.vector.tensor_tensor(
-                out=rows[:].rearrange("p (u j e) -> p u j e", u=2, e=2),
-                in0=acc[:].rearrange("p (j u e) -> p u j e", u=2, e=2),
-                in1=h_raw[a, g][:, i, :].rearrange("p (j u e) -> p u j e", u=2, e=2),
+                out=rows[:].rearrange("p (u q r e) -> p q u r e", u=2, r=8, e=2),
+                in0=acc[:].rearrange("p (q u e r) -> p q u r e", u=2, r=8, e=2),
+                in1=h_raw[a, g][:, i, :].rearrange("p (q u e r) -> p q u r e", u=2, r=8, e=2),
                 op=ALU.add,
             )
             q_rows[a, g, i] = rows
@@ -163,7 +173,9 @@ def tile_multiplicative_quadratic_step_k4_kernel(
                 for u in range(2):
                     nc.tensor.transpose(bank[:, 2 * i + u, :], words[:, u * P : (u + 1) * P], ident[:])
             if half == 0:
-                q_packed[a, g] = new_packed("q_packed_%d_%d" % (a, g))
+                q_packed[a, g] = keep.tile(
+                    [P, 4 * G], BF16, name="q_packed_%d_%d" % (a, g), tag="h_raw_%d_%d" % (a, g), align_bytes=64
+                )
             dst = q_packed[a, g][:].bitcast(F32).rearrange("p (t i j u) -> p t i j u", t=4, i=4, u=2)
             nc.scalar.copy(
                 out=dst[:, :, 2 * half : 2 * half + 2, :, :],
@@ -176,34 +188,64 @@ def tile_multiplicative_quadratic_step_k4_kernel(
         def x_sort(g):
             t = keep.tile([P, PASSES, G], I32, name="x_codes_%d" % g, align_bytes=64)
             nc.vector.tensor_copy(
-                out=t[:].rearrange("p c (t j i) -> p c j t i", t=4, i=4),
-                in_=x_raw[g][:].rearrange("p c (j i t) -> p c j t i", t=4, i=4),
+                out=t[:].rearrange("p c (t q r) -> p c t q r", t=4, r=8),
+                in_=x_raw[g][:].rearrange("p c (q t r) -> p c t q r", t=4, r=8),
             )
-            s = keep.tile([P, PASSES, G], U8, name="x_scales_%d" % g, align_bytes=64)
+            x_codes[g] = t
+
+        def x_sort_scales():
             nc.vector.tensor_copy(
-                out=s[:].rearrange("p c (t j i) -> p c j t i", t=4, i=16),
-                in_=x_plane[:, :, g * G : (g + 1) * G].rearrange("p c (j i t) -> p c j t i", t=4, i=16),
+                out=x_sorted[:].bitcast(I32).rearrange("p c (g t q w) -> p c g t q w", g=GROUPS, t=4, w=2),
+                in_=x_plane[:].bitcast(I32).rearrange("p c (g q t w) -> p c g t q w", g=GROUPS, t=4, w=2),
             )
-            x_codes[g] = (t, s)
 
-        def u_tile(g, t):
-            acc = mm_bank("u_acc_%d_%d" % (g, t))
-            for c in range(PASSES):
-                nc.tensor.matmul_mx(
-                    out=acc[:],
-                    lhsT=x_codes[g][0][:, c, t * P : (t + 1) * P].bitcast(FP8X4),
-                    lhsT_scale=x_codes[g][1][:, c, t * P : (t + 1) * P],
-                    rhs=w_mx[c][0][:].bitcast(FP8X4),
-                    rhs_scale=w_mx[c][1][:],
-                    start=(c == 0),
-                    stop=(c == PASSES - 1),
-                )
-            if t == 0:
-                u_rows[g] = work.tile([P, 4, M], BF16, name="u_rows_%d" % g, tag="u_rows", bufs=2)
-            nc.scalar.activation(out=u_rows[g][:, t, :], in_=acc[:], func=ACT.Identity, bias=anchor_sb[:, g, t : t + 1])
+        def w_pack(h, c):
+            if c == 0:
+                packed["w", h] = new_packed("packed_w_%d" % h)
+            dst = packed["w", h][:, 4 * c * HALF : 4 * (c + 1) * HALF]
+            interleave("s", dst, w_raw[:, c, :, h * HALF : (h + 1) * HALF], 0, HALF)
 
-        def u_quant(g):
-            u_mx[g] = quantize("u_%d" % g, packed["u", g, 0])
+        def w_quant(h):
+            w_mx[h] = quantize("w_%d" % h, packed["w", h])
+
+        def u_group(g, h):
+            u_rows[g, h] = work.tile([P, 4, HALF], BF16, name="u_rows_%d_%d" % (g, h), tag="u_rows", bufs=3)
+            for u in range(2):
+                acc = mm_bank("u_acc_%d_%d_%d" % (g, h, u))
+                for e in range(2):
+                    t = 2 * u + e
+                    for c in range(PASSES):
+                        nc.tensor.matmul_mx(
+                            out=acc[:, e * HALF : (e + 1) * HALF],
+                            lhsT=x_codes[g][:, c, t * P : (t + 1) * P].bitcast(FP8X4),
+                            lhsT_scale=x_sorted[:, c, g * G + t * P : g * G + (t + 1) * P],
+                            rhs=w_mx[h][0][:, c * HALF : (c + 1) * HALF].bitcast(FP8X4),
+                            rhs_scale=w_mx[h][1][:, c * HALF : (c + 1) * HALF],
+                            start=(c == 0),
+                            stop=(c == PASSES - 1),
+                        )
+                for e in range(2):
+                    t = 2 * u + e
+                    col = ANCHOR_COL + 4 * g + t
+                    nc.scalar.activation(
+                        out=u_rows[g, h][:, t, :],
+                        in_=acc[:, e * HALF : (e + 1) * HALF],
+                        func=ACT.Identity,
+                        bias=coef[:, col : col + 1],
+                    )
+
+        def u_pack(g, h, engine):
+            t = work.tile([P, 4 * HALF], BF16, name="packed_u_%d_%d" % (g, h), tag="packed_u", bufs=3, align_bytes=64)
+            interleave(engine, t, u_rows[g, h], 0, HALF)
+            packed["u", g, h] = t
+
+        def u_quant(g, h):
+            if h == 0:
+                u_mx[g] = new_mx("u_%d" % g)
+            cols = slice(h * HALF, (h + 1) * HALF)
+            nc.vector.quantize_mx(
+                out=u_mx[g][0][:, cols].bitcast(FP8X4), scales=u_mx[g][1][:, cols], in_=packed["u", g, h][:]
+            )
 
         def v_tile(a, mt):
             acc = mm_bank("v_acc_%d_%d" % (a, mt))
@@ -248,89 +290,95 @@ def tile_multiplicative_quadratic_step_k4_kernel(
 
         def y_quant(a, mt):
             if mt == 0:
-                y_mx[a] = new_mx("y_%d" % a)
-            codes, scales = y_mx[a]
+                y_codes[a] = keep.tile([P, M], U32, name="y_codes_%d" % a, align_bytes=64)
             cols = slice(mt * P, (mt + 1) * P)
-            nc.vector.quantize_mx(out=codes[:, cols].bitcast(FP8X4), scales=scales[:, cols], in_=y_packed[a, mt][:])
+            scales = y_first[:, cols] if a == 0 else y_rest[4 * (a - 1) :, cols]
+            nc.vector.quantize_mx(out=y_codes[a][:, cols].bitcast(FP8X4), scales=scales, in_=y_packed[a, mt][:])
             if mt % 2 == 1:
                 dst = out_1[a, :, (mt - 1) * P : (mt + 1) * P, :].rearrange("p m t -> p (m t)")
-                nc.sync.dma_start(out=dst.bitcast(I32), in_=codes[:, (mt - 1) * P : (mt + 1) * P].bitcast(I32))
-            if mt == TILES - 1:
+                nc.sync.dma_start(out=dst.bitcast(I32), in_=y_codes[a][:, (mt - 1) * P : (mt + 1) * P].bitcast(I32))
+            if (a, mt) == (0, TILES - 1):
                 for quad in range(4):
-                    queue = nc.scalar if a == GROUPS - 1 and quad % 2 == 1 else nc.sync
+                    nc.sync.dma_start(
+                        out=out_2[0, 4 * quad : 4 * quad + 4, :].bitcast(I32),
+                        in_=y_first[32 * quad : 32 * quad + 4, :].bitcast(I32),
+                    )
+            if (a, mt) == (GROUPS - 1, TILES - 1):
+                for quad in range(4):
+                    queue = nc.scalar if quad % 2 == 0 else nc.sync
                     queue.dma_start(
-                        out=out_2[a, 4 * quad : 4 * quad + 4, :].bitcast(I32),
-                        in_=scales[32 * quad : 32 * quad + 4, :].bitcast(I32),
+                        out=out_2[1:, 4 * quad : 4 * quad + 4, :].bitcast(I32),
+                        in_=y_rest[32 * quad : 32 * quad + 8, :].bitcast(I32),
                     )
 
-        l_scales = keep.tile([P, PASSES, D], U8, name="l_scales", align_bytes=64)
+        y_codes = {}
+        y_first = keep.tile([P, M], U8, name="y_scales_first", align_bytes=64)
+        y_rest = keep.tile([P, M], U8, name="y_scales_rest", align_bytes=64)
+
+        l_first = keep.tile([P, PASSES, G], U8, name="l_first", align_bytes=64)
+        l_rest = keep.tile([P, PASSES, D - G], U8, name="l_rest", align_bytes=64)
         x_plane = keep.tile([P, PASSES, D], U8, name="x_plane", align_bytes=64)
-        nc.vector.memset(l_scales[:].bitcast(I32), 0)
+        nc.vector.memset(l_first[:].bitcast(I32), 0)
         warm = keep.tile([P, 2], F32, name="warm")
         nc.vector.memset(warm[:, 0:1], 0.0)
+        nc.vector.memset(l_rest[:].bitcast(I32), 0)
         nc.vector.memset(x_plane[:].bitcast(I32), 0)
         load_r(0, 0)
-        load_scale_rows(nc.scalar, l_scales, L_scales)
-        load_l(0)
+        load_scale_rows(nc.scalar, l_first, L_scales, slice(0, G))
         load_r(1, 0)
+        load_l(0)
         load_h(0, 0)
 
         ident = keep.tile([P, P], F32, name="ident")
         coef_bf = keep.tile([P, P], BF16, name="coef_bf")
         coef_rows = keep.tile([P, P], F32, name="coef_rows")
-        anchor_sb = keep.tile([P, GROUPS, 4], BF16, name="anchor_sb")
+        make_identity(nc, ident[:])
         nc.gpsimd.dma_start(out=coef_bf[0:4, :], in_=rate.rearrange("(i p) -> i p", p=P))
         nc.gpsimd.dma_start(out=coef_bf[32:36, :], in_=shift.rearrange("(i p) -> i p", p=P))
-        nc.gpsimd.dma_start(out=anchor_sb[:], in_=anchor.rearrange("(g p t) -> p g t", p=P, t=4))
+        for g in range(GROUPS):
+            nc.gpsimd.dma_start(
+                out=coef_bf[ANCHOR_COL + 4 * g : ANCHOR_COL + 4 * g + 4, :].rearrange("t (q r) -> t q r", r=8),
+                in_=anchor[g * G : (g + 1) * G].rearrange("(q t r) -> t q r", t=4, r=8),
+            )
         nc.gpsimd.memset(coef_rows[:], 0.0)
         nc.scalar.activation(out=warm[:, 1:2], in_=warm[:, 0:1], func=ACT.Exp)
-        make_identity(nc, ident[:])
         nc.gpsimd.tensor_scalar(
             out=coef_rows[0:4, :], in0=coef_bf[0:4, :], scalar1=-1.0, scalar2=0.0, op0=ALU.mult, op1=ALU.add
         )
         nc.gpsimd.tensor_scalar(
             out=coef_rows[32:36, :], in0=coef_bf[32:36, :], scalar1=1.0, scalar2=0.0, op0=ALU.mult, op1=ALU.add
         )
+        nc.gpsimd.tensor_scalar(
+            out=coef_rows[64:76, :], in0=coef_bf[64:76, :], scalar1=1.0, scalar2=0.0, op0=ALU.mult, op1=ALU.add
+        )
 
         load_r(0, 1)
         load_l(1)
+        load_scale_rows(nc.sync, l_rest, L_scales, slice(G, D))
         load_h(1, 0)
         load_r(1, 1)
         load_l(2)
         load_h(2, 0)
-        load_w(0)
-        load_h(0, 1)
-        load_w(1)
-        load_scale_rows(nc.sync, x_plane, X_scales)
-        load_h(1, 1)
-        load_x(0)
         load_r(0, 2)
-        load_h(2, 1)
+        load_h(0, 1)
         load_r(1, 2)
-        load_x(1)
+        load_h(1, 1)
+        load_w()
+        load_h(2, 1)
+        load_scale_rows(nc.sync, x_plane, X_scales, slice(0, D))
+        load_x(0)
         load_h(0, 2)
-        load_x(2)
+        load_x(1)
         load_h(1, 2)
+        load_x(2)
         load_h(2, 2)
 
-        coef = keep.tile([P, 36], F32, name="coef")
+        coef = keep.tile([P, 76], F32, name="coef")
 
         def make_coef():
             bank = turn_bank("coef_turn")
             nc.tensor.transpose(bank[:, 0, :], coef_rows[:], ident[:])
-            nc.scalar.copy(out=coef[:], in_=bank[:, 0, 0:36])
-
-        def u_group(g):
-            for t in range(4):
-                u_tile(g, t)
-
-        def u_pack_s(g):
-            packed["u", g, 0] = new_packed("packed_u_%d" % g)
-            interleave("s", packed["u", g, 0], u_rows[g], U_V, G)
-
-        def u_pack_v(g):
-            if U_V > 0:
-                interleave("v", packed["u", g, 0], u_rows[g], 0, U_V)
+            nc.scalar.copy(out=coef[:], in_=bank[:, 0, 0:76])
 
         def turn(a, g):
             q_turn(a, g, 0)
@@ -346,68 +394,101 @@ def tile_multiplicative_quadratic_step_k4_kernel(
         for c in range(PASSES):
             pack(("r", c, 0), r_raw[c, 0], HEAD_V)
             quant_r(c, 0)
-            for i in range(TILES):
+            for i in range(HEAD_TILES):
                 q_pass(0, 0, i, c)
         pack(("r", 0, 1), r_raw[0, 1], SIDE_V)
-        for i in range(TILES):
+        for i in range(HEAD_TILES):
             q_add(0, 0, i)
+        for i in range(HEAD_TILES, TILES):
+            q_tile(0, 0, i)
         unit(1, 0, [None, lambda: quant_r(0, 1)])
         pack(("r", 1, 1), r_raw[1, 1], SIDE_V)
         turn(0, 0)
-        make_coef()
-        unit(2, 0, [None, lambda: quant_r(1, 1), None, lambda: q_quant(0, 0)])
-        pack(("w", 0, 0), w_raw[0], SIDE_W, W_ENG)
+        unit(2, 0, [None, lambda: quant_r(1, 1)])
         turn(1, 0)
-        unit(0, 1, [None, lambda: quant_w(0), None, lambda: q_quant(1, 0)])
-        pack(("w", 1, 0), w_raw[1], SIDE_W, W_ENG)
-        turn(2, 0)
-        unit(1, 1, [None, lambda: quant_w(1), lambda: x_sort(0), lambda: q_quant(2, 0)])
         pack(("r", 0, 2), r_raw[0, 2], SIDE_V)
-        turn(0, 1)
-        unit(2, 1, [None, lambda: quant_r(0, 2), None, lambda: q_quant(0, 1)])
+        unit(0, 1, [None, lambda: q_quant(0, 0), None, lambda: quant_r(0, 2)])
+        turn(2, 0)
+        make_coef()
         pack(("r", 1, 2), r_raw[1, 2], SIDE_V2)
+        unit(1, 1, [None, None, None, lambda: quant_r(1, 2)])
+        turn(0, 1)
+        w_pack(0, 0)
+        w_pack(0, 1)
+        unit(2, 1, [None, x_sort_scales, None, lambda: x_sort(0)])
+        w_quant(0)
         for a in range(GROUPS):
             load_z(a)
         turn(1, 1)
-        u_group(0)
-        x_sort(1)
-        quant_r(1, 2)
-        q_quant(1, 1)
+        w_pack(1, 0)
+        unit(0, 2, [None, None, lambda: x_sort(1), lambda: q_quant(0, 1)])
+        u_group(0, 0)
         turn(2, 1)
-        u_pack_s(0)
-        unit(0, 2, [None, lambda: u_pack_v(0), lambda: q_quant(2, 1), lambda: u_quant(0)])
-        u_group(1)
-        x_sort(2)
+        u_pack(0, 0, "s")
+        unit(1, 2, [lambda: x_sort(2), None, lambda: q_quant(1, 0), lambda: u_quant(0, 0)])
+        u_group(1, 0)
+        u_group(2, 0)
         turn(0, 2)
-        u_pack_s(1)
-        unit(1, 2, [None, lambda: u_pack_v(1), lambda: q_quant(0, 2), lambda: u_quant(1)])
-        u_group(2)
-        u_pack_s(2)
+        u_pack(1, 0, "v")
+        q_quant(1, 1)
+        u_pack(2, 0, "v")
+        u_quant(1, 0)
+        u_quant(2, 0)
+        q_quant(0, 2)
+        w_pack(1, 1)
+        unit(2, 2)
         turn(1, 2)
-        u_pack_v(2)
-        unit(2, 2, [lambda: u_quant(2), None, lambda: q_quant(1, 2)])
 
-        steps = [(a, mt) for a in range(GROUPS) for mt in range(TILES)]
+        pairs = [[(a, 2 * h), (a, 2 * h + 1)] for h in range(2) for a in range(GROUPS)]
 
-        def finish(pair):
+        def multiply(pair):
+            for step in pair:
+                v_tile(*step)
+
+        def turn_e(pair):
             for step in pair:
                 e_turn(*step)
-            for step in pair:
-                y_pack(*step, "s" if step[1] % 2 == 0 else "v")
+
+        def planes(pair, first=YE):
+            y_pack(*pair[0], first)
+            y_pack(*pair[1], "v")
             for step in pair:
                 y_quant(*step)
 
-        pairs = [steps[s : s + 2] for s in range(0, len(steps), 2)]
-        for n, pair in enumerate(pairs[:-1]):
-            for step in pair:
-                v_tile(*step)
-            if n == 0:
-                turn(2, 2)
-            else:
-                finish(pairs[n - 1])
-            if n == 1:
-                q_quant(2, 2)
-        v_tile(*pairs[-1][0])
-        finish(pairs[-2])
-        v_tile(*pairs[-1][1])
-        finish(pairs[-1])
+        def finish(pair, first=YE):
+            turn_e(pair)
+            planes(pair, first)
+
+        multiply(pairs[0])
+        q_quant(1, 2)
+        w_quant(1)
+        turn(2, 2)
+        q_quant(2, 0)
+        multiply(pairs[1])
+        q_quant(2, 1)
+        q_quant(2, 2)
+        u_group(0, 1)
+        u_group(1, 1)
+        u_pack(0, 1, UE1)
+        turn_e(pairs[0])
+        u_group(2, 1)
+        u_pack(1, 1, UE1)
+        u_quant(0, 1)
+        u_quant(1, 1)
+        multiply(pairs[2])
+        u_pack(2, 1, UE1)
+        y_pack(*pairs[0][1], "v")
+        u_quant(2, 1)
+        y_pack(*pairs[0][0], "s")
+        turn_e(pairs[1])
+        for step in pairs[0]:
+            y_quant(*step)
+        planes(pairs[1])
+        multiply(pairs[3])
+        finish(pairs[2])
+        multiply(pairs[4])
+        finish(pairs[3])
+        v_tile(*pairs[5][0])
+        finish(pairs[4], "v")
+        v_tile(*pairs[5][1])
+        finish(pairs[5])

from contextlib import ExitStack

import concourse.mybir as mybir
from concourse.masks import make_identity

D, K, J, M = 1536, 1024, 1024, 512
FLOPS = 2 * D * K * D + 2 * D * J * M + 2 * D * D * M

F32 = mybir.dt.float32
BF16 = mybir.dt.bfloat16
I32 = mybir.dt.int32
U32 = mybir.dt.uint32
U8 = mybir.dt.uint8
FP8X4 = mybir.dt.float8_e4m3fn_x4
FP4X4 = mybir.dt.float4_e2m1fn_x4
ALU = mybir.AluOpType
ACT = mybir.ActivationFunctionType

P = 128
G = 512
PASSES = K // G
GROUPS = D // G
TILES = G // P
HEAD_V = 336
U_V = 256
W_ENG = "s"
Y_ENG = "v"
MM_BANKS = 5
HEAD_TILES = 2
HALF = M // 2
ANCHOR_COL = 64
UE0 = "s"
UE1 = "v"
YE = "s"
SIDE_V = 0
SIDE_W = 0
SIDE_V2 = 128
RUN = 2
Y_LAST = 8


def tile_multiplicative_quadratic_step_k4_kernel(
    tc, L_words, L_scales, R, H, X_words, X_scales, W, anchor, Z, rate, shift, out_0, out_1, out_2
):
    nc = tc.nc
    with ExitStack() as ctx:
        keep = ctx.enter_context(tc.tile_pool(name="keep", bufs=1))
        work = ctx.enter_context(tc.tile_pool(name="work", bufs=4))
        psum = ctx.enter_context(tc.psum_pool(name="psum", bufs=1))
        ctx.enter_context(tc.manual_schedule())

        r_raw, h_raw, x_raw, z_raw, l_codes = {}, {}, {}, {}, {}
        w_raw = keep.tile([P, PASSES, 4, M], BF16, name="w_raw")
        x_sorted = keep.tile([P, PASSES, D], U8, name="x_sorted", align_bytes=64)
        q_acc = {}
        r_mx, w_mx, q_mx, u_mx, y_mx = {}, {}, {}, {}, {}
        x_codes, q_rows, q_packed, u_rows, u_packed, e_rows, y_rows, y_packed, packed = {}, {}, {}, {}, {}, {}, {}, {}, {}

        def load_rows(name, rows, tag=None):
            t = keep.tile([P, 4, G], BF16, name=name, tag=tag or name, align_bytes=64)
            nc.sync.dma_start(out=t[:], in_=rows)
            return t

        def load_r(c, g):
            rows = R[c * G : (c + 1) * G, g * G : (g + 1) * G]
            r_raw[c, g] = load_rows("r_raw_%d_%d" % (c, g), rows.rearrange("(p t) n -> p t n", t=4))

        def load_w():
            nc.sync.dma_start(out=w_raw[:], in_=W.rearrange("(c p t) n -> p c t n", p=P, t=4))

        def load_z(a):
            z_raw[a] = load_rows("z_raw_%d" % a, Z[a * G : (a + 1) * G, :].rearrange("(p t) n -> p t n", t=4), "r_raw_0_%d" % a)

        def load_h(a, g):
            rows = H[a * G : (a + 1) * G, g * G : (g + 1) * G]
            h_raw[a, g] = load_rows("h_raw_%d_%d" % (a, g), rows.rearrange("(i p) n -> p i n", p=P))

        def load_l(a):
            t = keep.tile([P, PASSES, 2 * G], U8, name="l_codes_%d" % a, align_bytes=64)
            src = L_words[:, :, 2 * a * G : 2 * (a + 1) * G].rearrange("c p n -> p c n")
            nc.sync.dma_start(out=t[:].bitcast(I32), in_=src.bitcast(I32))
            l_codes[a] = t

        def load_x(g):
            t = keep.tile([P, PASSES, G], I32, name="x_raw_%d" % g)
            src = X_words.rearrange("c p n t -> p c (n t)")[:, :, 4 * g * G : 4 * (g + 1) * G]
            nc.sync.dma_start(out=t[:], in_=src.bitcast(I32))
            x_raw[g] = t

        def load_scale_rows(queue, plane, scales, cols):
            for quad in range(4):
                src = scales[:, 4 * quad : 4 * quad + 4, cols].rearrange("c r n -> r c n")
                queue.dma_start(out=plane[32 * quad : 32 * quad + 4, :, :].bitcast(I32), in_=src.bitcast(I32))

        def interleave(engine, dst, src, lo, hi):
            out = dst[:, 4 * lo : 4 * hi].rearrange("p (c i t) -> p c t i", i=4, t=4)
            in_ = src[:, :, lo:hi].rearrange("p t (c i) -> p c t i", i=4)
            if engine == "v":
                nc.vector.tensor_copy(out=out, in_=in_)
            elif engine == "s":
                nc.scalar.copy(out=out, in_=in_)
            else:
                nc.gpsimd.tensor_scalar(out=out, in0=in_, scalar1=1.0, scalar2=0.0, op0=ALU.mult, op1=ALU.add)

        def new_packed(name):
            return work.tile([P, 4 * G], BF16, name=name, tag="packed", bufs=3, align_bytes=64)

        def new_mx(name):
            codes = keep.tile([P, G], U32, name=name + "_codes", align_bytes=64)
            scales = keep.tile([P, G], U8, name=name + "_scales", align_bytes=64)
            return codes, scales

        def quantize(name, src):
            codes, scales = new_mx(name)
            nc.vector.quantize_mx(out=codes[:].bitcast(FP8X4), scales=scales[:], in_=src[:])
            return codes, scales

        def mm_bank(name):
            return psum.tile([P, G], F32, name=name, tag="mm", bufs=MM_BANKS)

        def turn_bank(name):
            return psum.tile([P, 4, P], F32, name=name, tag="turn", bufs=8 - MM_BANKS)

        def pack(key, raw, on_vector, other="s"):
            packed[key] = new_packed("packed_%s_%d_%d" % key)
            if on_vector < G:
                interleave(other, packed[key], raw, on_vector, G)
            if on_vector > 0:
                interleave("v", packed[key], raw, 0, on_vector)

        def quant_r(c, g):
            r_mx[c, g] = quantize("r_%d_%d" % (c, g), packed["r", c, g])

        def l_scale_cols(a, c, i):
            if a == 0:
                return l_first[:, c, i * P : (i + 1) * P]
            return l_rest[:, c, (a - 1) * G + i * P : (a - 1) * G + (i + 1) * P]

        def q_pass(a, g, i, c):
            if c == 0:
                q_acc[a, g, i] = mm_bank("q_acc_%d_%d_%d" % (a, g, i))
            acc = q_acc[a, g, i]
            nc.tensor.matmul_mx(
                out=acc[:],
                lhsT=l_codes[a][:, c, 2 * i * P : 2 * (i + 1) * P].bitcast(FP4X4),
                lhsT_scale=l_scale_cols(a, c, i),
                rhs=r_mx[c, g][0][:].bitcast(FP8X4),
                rhs_scale=r_mx[c, g][1][:],
                start=(c == 0),
                stop=(c == PASSES - 1),
            )

        def q_tile(a, g, i):
            for c in range(PASSES):
                q_pass(a, g, i, c)
            q_add(a, g, i)

        def q_add(a, g, i):
            acc = q_acc[a, g, i]
            rows = work.tile([P, G], BF16, name="q_rows_%d_%d_%d" % (a, g, i), tag="q_rows", bufs=8)
            nc.vector.tensor_tensor(
                out=rows[:].rearrange("p (u q r e) -> p q u r e", u=2, r=8, e=2),
                in0=acc[:].rearrange("p (q u e r) -> p q u r e", u=2, r=8, e=2),
                in1=h_raw[a, g][:, i, :].rearrange("p (q u e r) -> p q u r e", u=2, r=8, e=2),
                op=ALU.add,
            )
            q_rows[a, g, i] = rows

        def q_turn(a, g, half):
            bank = turn_bank("q_turn_%d_%d_%d" % (a, g, half))
            for i in range(2):
                words = q_rows[a, g, 2 * half + i][:].bitcast(F32)
                for u in range(2):
                    nc.tensor.transpose(bank[:, 2 * i + u, :], words[:, u * P : (u + 1) * P], ident[:])
            if half == 0:
                q_packed[a, g] = keep.tile(
                    [P, 4 * G], BF16, name="q_packed_%d_%d" % (a, g), tag="h_raw_%d_%d" % (a, g), align_bytes=64
                )
            dst = q_packed[a, g][:].bitcast(F32).rearrange("p (t i j u) -> p t i j u", t=4, i=4, u=2)
            nc.scalar.copy(
                out=dst[:, :, 2 * half : 2 * half + 2, :, :],
                in_=bank[:].rearrange("p (i u) (j t) -> p t i j u", u=2, t=4),
            )

        def q_quant(a, g):
            q_mx[a, g] = quantize("q_%d_%d" % (a, g), q_packed[a, g])

        def x_sort(g):
            t = keep.tile([P, PASSES, G], I32, name="x_codes_%d" % g, align_bytes=64)
            nc.vector.tensor_copy(
                out=t[:].rearrange("p c (t q r) -> p c t q r", t=4, r=8),
                in_=x_raw[g][:].rearrange("p c (q t r) -> p c t q r", t=4, r=8),
            )
            x_codes[g] = t

        def x_sort_scales():
            nc.vector.tensor_copy(
                out=x_sorted[:].bitcast(I32).rearrange("p c (g t q w) -> p c g t q w", g=GROUPS, t=4, w=2),
                in_=x_plane[:].bitcast(I32).rearrange("p c (g q t w) -> p c g t q w", g=GROUPS, t=4, w=2),
            )

        def w_pack(h, c):
            if c == 0:
                packed["w", h] = new_packed("packed_w_%d" % h)
            dst = packed["w", h][:, 4 * c * HALF : 4 * (c + 1) * HALF]
            interleave("s", dst, w_raw[:, c, :, h * HALF : (h + 1) * HALF], 0, HALF)

        def w_quant(h):
            w_mx[h] = quantize("w_%d" % h, packed["w", h])

        def u_group(g, h):
            u_rows[g, h] = work.tile([P, 4, HALF], BF16, name="u_rows_%d_%d" % (g, h), tag="u_rows", bufs=3)
            for u in range(2):
                acc = mm_bank("u_acc_%d_%d_%d" % (g, h, u))
                for e in range(2):
                    t = 2 * u + e
                    for c in range(PASSES):
                        nc.tensor.matmul_mx(
                            out=acc[:, e * HALF : (e + 1) * HALF],
                            lhsT=x_codes[g][:, c, t * P : (t + 1) * P].bitcast(FP8X4),
                            lhsT_scale=x_sorted[:, c, g * G + t * P : g * G + (t + 1) * P],
                            rhs=w_mx[h][0][:, c * HALF : (c + 1) * HALF].bitcast(FP8X4),
                            rhs_scale=w_mx[h][1][:, c * HALF : (c + 1) * HALF],
                            start=(c == 0),
                            stop=(c == PASSES - 1),
                        )
                for e in range(2):
                    t = 2 * u + e
                    col = ANCHOR_COL + 4 * g + t
                    nc.scalar.activation(
                        out=u_rows[g, h][:, t, :],
                        in_=acc[:, e * HALF : (e + 1) * HALF],
                        func=ACT.Identity,
                        bias=coef[:, col : col + 1],
                    )

        def u_pack(g, h, engine):
            t = work.tile([P, 4 * HALF], BF16, name="packed_u_%d_%d" % (g, h), tag="packed_u", bufs=3, align_bytes=64)
            interleave(engine, t, u_rows[g, h], 0, HALF)
            packed["u", g, h] = t

        def u_quant(g, h):
            if h == 0:
                u_mx[g] = new_mx("u_%d" % g)
            cols = slice(h * HALF, (h + 1) * HALF)
            nc.vector.quantize_mx(
                out=u_mx[g][0][:, cols].bitcast(FP8X4), scales=u_mx[g][1][:, cols], in_=packed["u", g, h][:]
            )

        def v_tile(a, mt):
            acc = mm_bank("v_acc_%d_%d" % (a, mt))
            cols = slice(mt * P, (mt + 1) * P)
            for g in range(GROUPS):
                nc.tensor.matmul_mx(
                    out=acc[:],
                    lhsT=u_mx[g][0][:, cols].bitcast(FP8X4),
                    lhsT_scale=u_mx[g][1][:, cols],
                    rhs=q_mx[a, g][0][:].bitcast(FP8X4),
                    rhs_scale=q_mx[a, g][1][:],
                    start=(g == 0),
                    stop=(g == GROUPS - 1),
                )
            rows = work.tile([P, G], F32, name="e_rows_%d_%d" % (a, mt), tag="e_rows", bufs=6)
            nc.scalar.activation(
                out=rows[:], in_=acc[:], func=ACT.Exp, bias=coef[:, 32 + mt : 33 + mt], scale=coef[:, mt : mt + 1]
            )
            e_rows[a, mt] = rows

        def e_turn(a, mt):
            bank = turn_bank("e_turn_%d_%d" % (a, mt))
            for t in range(4):
                nc.tensor.transpose(bank[:, t, :], e_rows[a, mt][:, t * P : (t + 1) * P], ident[:])
            cols = slice(mt * P, (mt + 1) * P)
            if mt % 2 == 0:
                y_rows[a, mt // 2] = work.tile([P, 4, 2 * P], F32, name="y_rows_%d_%d" % (a, mt), tag="y_rows", bufs=3)
            rows = y_rows[a, mt // 2]
            half = slice((mt % 2) * P, (mt % 2 + 1) * P)
            nc.vector.tensor_tensor(out=rows[:, :, half], in0=bank[:], in1=z_raw[a][:, :, cols], op=ALU.mult)
            if (a, mt // 2) == (GROUPS - 1, 1):
                dst = out_0[a * G : (a + 1) * G, cols].rearrange("(p t) m -> p t m", t=4)
                nc.sync.dma_start(out=dst, in_=rows[:, :, half])
            elif mt % 2 == 1:
                dst = out_0[a * G : (a + 1) * G, (mt - 1) * P : (mt + 1) * P].rearrange("(p t) m -> p t m", t=4)
                nc.sync.dma_start(out=dst, in_=rows[:])

        def y_pack(a, mt, engine):
            t = work.tile([P, 4 * P], BF16, name="y_packed_%d_%d" % (a, mt), tag="y_packed", bufs=4, align_bytes=64)
            interleave(engine, t, y_rows[a, mt // 2][:, :, (mt % 2) * P : (mt % 2 + 1) * P], 0, P)
            y_packed[a, mt] = t

        def y_quant(a, mt):
            if mt == 0:
                y_codes[a] = keep.tile([P, M], U32, name="y_codes_%d" % a, align_bytes=64)
            cols = slice(mt * P, (mt + 1) * P)
            scales = y_first[:, cols] if a == 0 else y_rest[4 * (a - 1) :, cols]
            nc.vector.quantize_mx(out=y_codes[a][:, cols].bitcast(FP8X4), scales=scales, in_=y_packed[a, mt][:])
            if mt % 2 == 1:
                dst = out_1[a, :, (mt - 1) * P : (mt + 1) * P, :].rearrange("p m t -> p (m t)")
                nc.sync.dma_start(out=dst.bitcast(I32), in_=y_codes[a][:, (mt - 1) * P : (mt + 1) * P].bitcast(I32))
            if (a, mt) == (0, TILES - 1):
                for quad in range(4):
                    nc.sync.dma_start(
                        out=out_2[0, 4 * quad : 4 * quad + 4, :].bitcast(I32),
                        in_=y_first[32 * quad : 32 * quad + 4, :].bitcast(I32),
                    )
            if (a, mt) == (GROUPS - 1, TILES - 1):
                for quad in range(4):
                    queue = nc.scalar if quad % 2 == 0 else nc.sync
                    queue.dma_start(
                        out=out_2[1:, 4 * quad : 4 * quad + 4, :].bitcast(I32),
                        in_=y_rest[32 * quad : 32 * quad + 8, :].bitcast(I32),
                    )

        y_codes = {}
        y_first = keep.tile([P, M], U8, name="y_scales_first", align_bytes=64)
        y_rest = keep.tile([P, M], U8, name="y_scales_rest", align_bytes=64)

        l_first = keep.tile([P, PASSES, G], U8, name="l_first", align_bytes=64)
        l_rest = keep.tile([P, PASSES, D - G], U8, name="l_rest", align_bytes=64)
        x_plane = keep.tile([P, PASSES, D], U8, name="x_plane", align_bytes=64)
        nc.vector.memset(l_first[:].bitcast(I32), 0)
        warm = keep.tile([P, 2], F32, name="warm")
        nc.vector.memset(warm[:, 0:1], 0.0)
        nc.vector.memset(l_rest[:].bitcast(I32), 0)
        nc.vector.memset(x_plane[:].bitcast(I32), 0)
        load_r(0, 0)
        load_scale_rows(nc.scalar, l_first, L_scales, slice(0, G))
        load_r(1, 0)
        load_l(0)
        load_h(0, 0)

        ident = keep.tile([P, P], F32, name="ident")
        coef_bf = keep.tile([P, P], BF16, name="coef_bf")
        coef_rows = keep.tile([P, P], F32, name="coef_rows")
        make_identity(nc, ident[:])
        nc.gpsimd.dma_start(out=coef_bf[0:4, :], in_=rate.rearrange("(i p) -> i p", p=P))
        nc.gpsimd.dma_start(out=coef_bf[32:36, :], in_=shift.rearrange("(i p) -> i p", p=P))
        for g in range(GROUPS):
            nc.gpsimd.dma_start(
                out=coef_bf[ANCHOR_COL + 4 * g : ANCHOR_COL + 4 * g + 4, :].rearrange("t (q r) -> t q r", r=8),
                in_=anchor[g * G : (g + 1) * G].rearrange("(q t r) -> t q r", t=4, r=8),
            )
        nc.gpsimd.memset(coef_rows[:], 0.0)
        nc.scalar.activation(out=warm[:, 1:2], in_=warm[:, 0:1], func=ACT.Exp)
        nc.gpsimd.tensor_scalar(
            out=coef_rows[0:4, :], in0=coef_bf[0:4, :], scalar1=-1.0, scalar2=0.0, op0=ALU.mult, op1=ALU.add
        )
        nc.gpsimd.tensor_scalar(
            out=coef_rows[32:36, :], in0=coef_bf[32:36, :], scalar1=1.0, scalar2=0.0, op0=ALU.mult, op1=ALU.add
        )
        nc.gpsimd.tensor_scalar(
            out=coef_rows[64:76, :], in0=coef_bf[64:76, :], scalar1=1.0, scalar2=0.0, op0=ALU.mult, op1=ALU.add
        )

        load_r(0, 1)
        load_l(1)
        load_scale_rows(nc.sync, l_rest, L_scales, slice(G, D))
        load_h(1, 0)
        load_r(1, 1)
        load_l(2)
        load_h(2, 0)
        load_r(0, 2)
        load_h(0, 1)
        load_r(1, 2)
        load_h(1, 1)
        load_w()
        load_h(2, 1)
        load_scale_rows(nc.sync, x_plane, X_scales, slice(0, D))
        load_x(0)
        load_h(0, 2)
        load_x(1)
        load_h(1, 2)
        load_x(2)
        load_h(2, 2)

        coef = keep.tile([P, 76], F32, name="coef")

        def make_coef():
            bank = turn_bank("coef_turn")
            nc.tensor.transpose(bank[:, 0, :], coef_rows[:], ident[:])
            nc.scalar.copy(out=coef[:], in_=bank[:, 0, 0:76])

        def turn(a, g):
            q_turn(a, g, 0)
            q_turn(a, g, 1)

        def unit(a, g, side=()):
            side = list(side)
            for i in range(TILES):
                q_tile(a, g, i)
                if i < len(side) and side[i] is not None:
                    side[i]()

        for c in range(PASSES):
            pack(("r", c, 0), r_raw[c, 0], HEAD_V)
            quant_r(c, 0)
            for i in range(HEAD_TILES):
                q_pass(0, 0, i, c)
        pack(("r", 0, 1), r_raw[0, 1], SIDE_V)
        for i in range(HEAD_TILES):
            q_add(0, 0, i)
        for i in range(HEAD_TILES, TILES):
            q_tile(0, 0, i)
        unit(1, 0, [None, lambda: quant_r(0, 1)])
        pack(("r", 1, 1), r_raw[1, 1], SIDE_V)
        turn(0, 0)
        unit(2, 0, [None, lambda: quant_r(1, 1)])
        turn(1, 0)
        pack(("r", 0, 2), r_raw[0, 2], SIDE_V)
        unit(0, 1, [None, lambda: q_quant(0, 0), None, lambda: quant_r(0, 2)])
        turn(2, 0)
        make_coef()
        pack(("r", 1, 2), r_raw[1, 2], SIDE_V2)
        unit(1, 1, [None, None, None, lambda: quant_r(1, 2)])
        turn(0, 1)
        w_pack(0, 0)
        w_pack(0, 1)
        unit(2, 1, [None, x_sort_scales, None, lambda: x_sort(0)])
        w_quant(0)
        for a in range(GROUPS):
            load_z(a)
        turn(1, 1)
        w_pack(1, 0)
        unit(0, 2, [None, None, lambda: x_sort(1), lambda: q_quant(0, 1)])
        u_group(0, 0)
        turn(2, 1)
        u_pack(0, 0, "s")
        unit(1, 2, [lambda: x_sort(2), None, lambda: q_quant(1, 0), lambda: u_quant(0, 0)])
        u_group(1, 0)
        u_group(2, 0)
        turn(0, 2)
        u_pack(1, 0, "v")
        q_quant(1, 1)
        u_pack(2, 0, "v")
        u_quant(1, 0)
        u_quant(2, 0)
        q_quant(0, 2)
        w_pack(1, 1)
        unit(2, 2)
        turn(1, 2)

        pairs = [[(a, 2 * h), (a, 2 * h + 1)] for h in range(2) for a in range(GROUPS)]

        def multiply(pair):
            for step in pair:
                v_tile(*step)

        def turn_e(pair):
            for step in pair:
                e_turn(*step)

        def planes(pair, first=YE):
            y_pack(*pair[0], first)
            y_pack(*pair[1], "v")
            for step in pair:
                y_quant(*step)

        def finish(pair, first=YE):
            turn_e(pair)
            planes(pair, first)

        multiply(pairs[0])
        q_quant(1, 2)
        w_quant(1)
        turn(2, 2)
        q_quant(2, 0)
        multiply(pairs[1])
        q_quant(2, 1)
        q_quant(2, 2)
        u_group(0, 1)
        u_group(1, 1)
        u_pack(0, 1, UE1)
        turn_e(pairs[0])
        u_group(2, 1)
        u_pack(1, 1, UE1)
        u_quant(0, 1)
        u_quant(1, 1)
        multiply(pairs[2])
        u_pack(2, 1, UE1)
        y_pack(*pairs[0][1], "v")
        u_quant(2, 1)
        y_pack(*pairs[0][0], "s")
        turn_e(pairs[1])
        for step in pairs[0]:
            y_quant(*step)
        planes(pairs[1])
        multiply(pairs[3])
        finish(pairs[2])
        multiply(pairs[4])
        finish(pairs[3])
        v_tile(*pairs[5][0])
        finish(pairs[4], "v")
        v_tile(*pairs[5][1])
        finish(pairs[5])
